import numpy as np
CORES = [96,97,98,99,224,225,226,227,352,353,354,355,480,481,482,483]
N = 16
def setup_inputs(rng):
    return {"x1": rng.standard_normal((N, 128, 16), dtype=np.float32), "x2": rng.standard_normal((N, 128, 16), dtype=np.float32)}
def reference(x1, x2):
    out = []
    g = np.concatenate(list(x1), axis=1)
    out.append(np.broadcast_to(g, (N,) + g.shape))
    s = x2.sum(axis=0, dtype=np.float64).astype(x2.dtype)
    out.append(np.broadcast_to(s, (N,) + s.shape))
    return {"y1": out[0], "y2": out[1]}

@@ -1,0 +1,83 @@
+from concourse.bass import DstId, RemoteDMATransfer
+
+W = 16
+B = 4
+
+SCRATCH = {
+    "G1": ("sbuf", [128, 256], "float32"),
+    "X2": ("sbuf", [128, 16], "float32"),
+    "L2": ("sbuf", [128, 36], "float32"),
+    "Y2": ("sbuf", [128, 16], "float32"),
+}
+SEMAPHORES = ["ld", "s1", "s2", "s3a", "s3b", "sent", "st"]
+
+
+def rank_program(g, core, T, topo):
+    rank = T.rank_of(core)
+    if rank is None:
+        return
+    h, k = rank // 4, rank % 4
+    sem = T.sem
+
+    def at(hh, kk):
+        return T.cores[4 * hh + kk]
+
+    def did(dst):
+        rid, pid = topo.addr(dst, core)
+        return DstId(rid=rid, pnc=pid)
+
+    def piece(hh, kk):
+        j = 4 * hh + kk
+        return T.G1[:, W * j:W * (j + 1)]
+
+    def slot(s):
+        return T.L2[:, B * s:B * (s + 1)]
+
+    def send(srcs, dst_ap, dsts, mask, rsem, add=False):
+        return RemoteDMATransfer(dst_ids=[did(d) for d in dsts], dma_engine_mask=mask, remote_sem=rsem,
+                                 srcs=srcs, dsts=[dst_ap for d in dsts], alu_op=1 if add else 0)
+
+    rackp, cabp, diag = h ^ 1, 3 - h, h ^ 2
+    sibs = [at(h, j) for j in range(4) if j != k]
+
+    g.sync.dma_start(piece(h, k), T.x1[:]).then_inc(sem.ld, 16)
+    g.scalar.dma_start(T.X2[:], T.x2[:]).then_inc(sem.ld, 16)
+    g.wait_ge(sem.ld, 32)
+
+    g.remote_dma_fused([send([piece(h, k)], piece(h, k), [at(rackp, k), at(cabp, k)] + sibs, 0x00FF, sem.s1)],
+                       local_sem=sem.sent)
+    tr = []
+    for b in range(4):
+        src = T.X2[:, B * b:B * (b + 1)]
+        ids, aps = [did(at(cabp, b))], [slot(4 + k)]
+        if b != k:
+            ids.append(did(at(h, b)))
+            aps.append(slot(k))
+        tr.append(RemoteDMATransfer(dst_ids=ids, dma_engine_mask=0x3 << (2 * b), remote_sem=sem.s1,
+                                    srcs=[src], dsts=aps, alu_op=0))
+    g.remote_dma_fused(tr, local_sem=sem.sent)
+    g.wait_ge(sem.s1, 5 * 8 + 7 * 2)
+
+    g.remote_dma_fused([send([piece(rackp, k)], piece(rackp, k), [at(cabp, k)] + sibs, 0x00FF, sem.s2),
+                        send([piece(cabp, k)], piece(cabp, k), sibs, 0xFF00, sem.s2)],
+                       local_sem=sem.sent)
+    mine = [T.X2[:, B * k:B * (k + 1)]] + [slot(j) for j in range(4) if j != k] + [slot(4 + j) for j in range(4)]
+    g.remote_dma_fused([send(mine, slot(8), [at(rackp, k)], 0x00FF, sem.s2, add=True)], local_sem=sem.sent)
+    g.wait_ge(sem.s2, 8 + 6 * 8 + 8)
+
+    g.remote_dma_fused([send([piece(diag, k)], piece(diag, k), sibs, 0xFFFF, sem.s3a)], local_sem=sem.sent)
+    g.remote_dma_fused([send(mine + [slot(8)], T.Y2[:, B * k:B * (k + 1)], sibs + [at(rackp, k)], 0x00FF, sem.s3b,
+                             add=True)], local_sem=sem.sent)
+
+    g.sync.wait_ge(sem.ld, 32)
+    g.sync.wait_ge(sem.s1, 5 * 8 + 7 * 2)
+    g.sync.wait_ge(sem.s2, 8 + 6 * 8 + 8)
+    g.sync.wait_ge(sem.s3a, 3 * 16)
+    g.sync.dma_start(T.y1[:], T.G1[:]).then_inc(sem.st, 16)
+    g.scalar.wait_ge(sem.s3b, 4 * 8)
+    g.scalar.dma_start(T.y2[:], T.Y2[:]).then_inc(sem.st, 16)
+
+    g.wait_ge(sem.sent, (8 + 8) + (8 + 8 + 8) + (16 + 8))
+    g.wait_ge(sem.s3a, 3 * 16)
+    g.wait_ge(sem.s3b, 4 * 8)
+    g.wait_ge(sem.st, 32)

@@ -1,13 +1,12 @@
 from concourse.bass import DstId, RemoteDMATransfer
 
 W = 16
-B = 4
 
 SCRATCH = {
     "G1": ("sbuf", [128, 256], "float32"),
-    "X2": ("sbuf", [128, 16], "float32"),
-    "L2": ("sbuf", [128, 36], "float32"),
-    "Y2": ("sbuf", [128, 16], "float32"),
+    "X2": ("dram", [4, 128, 4], "float32"),
+    "L2": ("dram", [9, 128, 4], "float32"),
+    "Y2": ("dram", [4, 128, 4], "float32"),
 }
 SEMAPHORES = ["ld", "s1", "s2", "s3a", "s3b", "sent", "st"]
 
@@ -30,9 +29,6 @@ def rank_program(g, core, T, topo):
         j = 4 * hh + kk
         return T.G1[:, W * j:W * (j + 1)]
 
-    def slot(s):
-        return T.L2[:, B * s:B * (s + 1)]
-
     def send(srcs, dst_ap, dsts, mask, rsem, add=False):
         return RemoteDMATransfer(dst_ids=[did(d) for d in dsts], dma_engine_mask=mask, remote_sem=rsem,
                                  srcs=srcs, dsts=[dst_ap for d in dsts], alu_op=1 if add else 0)
@@ -48,30 +44,31 @@ def rank_program(g, core, T, topo):
                        local_sem=sem.sent)
     tr = []
     for b in range(4):
-        src = T.X2[:, B * b:B * (b + 1)]
-        ids, aps = [did(at(cabp, b))], [slot(4 + k)]
+        ids, aps = [did(at(cabp, b))], [T.L2[4 + k]]
         if b != k:
             ids.append(did(at(h, b)))
-            aps.append(slot(k))
+            aps.append(T.L2[k])
         tr.append(RemoteDMATransfer(dst_ids=ids, dma_engine_mask=0x3 << (2 * b), remote_sem=sem.s1,
-                                    srcs=[src], dsts=aps, alu_op=0))
+                                    srcs=[T.X2[b]], dsts=aps, alu_op=0))
     g.remote_dma_fused(tr, local_sem=sem.sent)
-    g.wait_ge(sem.s1, 5 * 8 + 7 * 2)
+    n1 = 5 * 8 + 7 * 2
+    g.wait_ge(sem.s1, n1)
 
     g.remote_dma_fused([send([piece(rackp, k)], piece(rackp, k), [at(cabp, k)] + sibs, 0x00FF, sem.s2),
                         send([piece(cabp, k)], piece(cabp, k), sibs, 0xFF00, sem.s2)],
                        local_sem=sem.sent)
-    mine = [T.X2[:, B * k:B * (k + 1)]] + [slot(j) for j in range(4) if j != k] + [slot(4 + j) for j in range(4)]
-    g.remote_dma_fused([send(mine, slot(8), [at(rackp, k)], 0x00FF, sem.s2, add=True)], local_sem=sem.sent)
-    g.wait_ge(sem.s2, 8 + 6 * 8 + 8)
+    mine = [T.X2[k]] + [T.L2[j] for j in range(4) if j != k] + [T.L2[4 + j] for j in range(4)]
+    g.remote_dma_fused([send(mine, T.L2[8], [at(rackp, k)], 0x00FF, sem.s2, add=True)], local_sem=sem.sent)
+    n2 = 8 + 6 * 8 + 8
+    g.wait_ge(sem.s2, n2)
 
     g.remote_dma_fused([send([piece(diag, k)], piece(diag, k), sibs, 0xFFFF, sem.s3a)], local_sem=sem.sent)
-    g.remote_dma_fused([send(mine + [slot(8)], T.Y2[:, B * k:B * (k + 1)], sibs + [at(rackp, k)], 0x00FF, sem.s3b,
-                             add=True)], local_sem=sem.sent)
+    g.remote_dma_fused([send(mine + [T.L2[8]], T.Y2[k], sibs + [at(rackp, k)], 0x00FF, sem.s3b, add=True)],
+                       local_sem=sem.sent)
 
     g.sync.wait_ge(sem.ld, 32)
-    g.sync.wait_ge(sem.s1, 5 * 8 + 7 * 2)
-    g.sync.wait_ge(sem.s2, 8 + 6 * 8 + 8)
+    g.sync.wait_ge(sem.s1, n1)
+    g.sync.wait_ge(sem.s2, n2)
     g.sync.wait_ge(sem.s3a, 3 * 16)
     g.sync.dma_start(T.y1[:], T.G1[:]).then_inc(sem.st, 16)
     g.scalar.wait_ge(sem.s3b, 4 * 8)

from concourse.bass import DstId, RemoteDMATransfer

W = 16

SCRATCH = {
    "G1": ("sbuf", [128, 256], "float32"),
    "X2": ("dram", [4, 128, 4], "float32"),
    "L2": ("dram", [9, 128, 4], "float32"),
    "Y2": ("dram", [4, 128, 4], "float32"),
}
SEMAPHORES = ["ld", "s1", "s2", "s3a", "s3b", "sent", "st"]


def rank_program(g, core, T, topo):
    rank = T.rank_of(core)
    if rank is None:
        return
    h, k = rank // 4, rank % 4
    sem = T.sem

    def at(hh, kk):
        return T.cores[4 * hh + kk]

    def did(dst):
        rid, pid = topo.addr(dst, core)
        return DstId(rid=rid, pnc=pid)

    def piece(hh, kk):
        j = 4 * hh + kk
        return T.G1[:, W * j:W * (j + 1)]

    def send(srcs, dst_ap, dsts, mask, rsem, add=False):
        return RemoteDMATransfer(dst_ids=[did(d) for d in dsts], dma_engine_mask=mask, remote_sem=rsem,
                                 srcs=srcs, dsts=[dst_ap for d in dsts], alu_op=1 if add else 0)

    rackp, cabp, diag = h ^ 1, 3 - h, h ^ 2
    sibs = [at(h, j) for j in range(4) if j != k]

    g.sync.dma_start(piece(h, k), T.x1[:]).then_inc(sem.ld, 16)
    g.scalar.dma_start(T.X2[:], T.x2[:]).then_inc(sem.ld, 16)
    g.wait_ge(sem.ld, 32)

    g.remote_dma_fused([send([piece(h, k)], piece(h, k), [at(rackp, k), at(cabp, k)] + sibs, 0x00FF, sem.s1)],
                       local_sem=sem.sent)
    tr = []
    for b in range(4):
        ids, aps = [did(at(cabp, b))], [T.L2[4 + k]]
        if b != k:
            ids.append(did(at(h, b)))
            aps.append(T.L2[k])
        tr.append(RemoteDMATransfer(dst_ids=ids, dma_engine_mask=0x3 << (2 * b), remote_sem=sem.s1,
                                    srcs=[T.X2[b]], dsts=aps, alu_op=0))
    g.remote_dma_fused(tr, local_sem=sem.sent)
    n1 = 5 * 8 + 7 * 2
    g.wait_ge(sem.s1, n1)

    g.remote_dma_fused([send([piece(rackp, k)], piece(rackp, k), [at(cabp, k)] + sibs, 0x00FF, sem.s2),
                        send([piece(cabp, k)], piece(cabp, k), sibs, 0xFF00, sem.s2)],
                       local_sem=sem.sent)
    mine = [T.X2[k]] + [T.L2[j] for j in range(4) if j != k] + [T.L2[4 + j] for j in range(4)]
    g.remote_dma_fused([send(mine, T.L2[8], [at(rackp, k)], 0x00FF, sem.s2, add=True)], local_sem=sem.sent)
    n2 = 8 + 6 * 8 + 8
    g.wait_ge(sem.s2, n2)

    g.remote_dma_fused([send([piece(diag, k)], piece(diag, k), sibs, 0xFFFF, sem.s3a)], local_sem=sem.sent)
    g.remote_dma_fused([send(mine + [T.L2[8]], T.Y2[k], sibs + [at(rackp, k)], 0x00FF, sem.s3b, add=True)],
                       local_sem=sem.sent)

    g.sync.wait_ge(sem.ld, 32)
    g.sync.wait_ge(sem.s1, n1)
    g.sync.wait_ge(sem.s2, n2)
    g.sync.wait_ge(sem.s3a, 3 * 16)
    g.sync.dma_start(T.y1[:], T.G1[:]).then_inc(sem.st, 16)
    g.scalar.wait_ge(sem.s3b, 4 * 8)
    g.scalar.dma_start(T.y2[:], T.Y2[:]).then_inc(sem.st, 16)

    g.wait_ge(sem.sent, (8 + 8) + (8 + 8 + 8) + (16 + 8))
    g.wait_ge(sem.s3a, 3 * 16)
    g.wait_ge(sem.s3b, 4 * 8)
    g.wait_ge(sem.st, 32)
